import numpy as np
import ml_dtypes


def mxq(x, axis, fmt="e4m3"):
    dtype, down = {"e4m3": (ml_dtypes.float8_e4m3fn, 7), "e5m2": (ml_dtypes.float8_e5m2, 14)}[fmt]
    v = np.moveaxis(np.asarray(x, np.float32).astype(ml_dtypes.bfloat16).astype(np.float64), axis, -1)
    blocks = v.reshape(v.shape[:-1] + (-1, 32))
    amax = np.abs(blocks).max(-1, keepdims=True)
    byte = np.maximum(np.where(amax > 0, np.frexp(amax)[1] - 1 + 127, 0) - down, 1)
    scale = np.exp2(byte - 127.0)
    codes = (blocks / scale).astype(np.float32).astype(dtype).astype(np.float64)
    return np.moveaxis((codes * scale).reshape(v.shape), -1, axis)


WIDE = False


def mx_kscale(k):
    if not WIDE:
        return np.ones(k)
    levels = np.array([10, -10, 5, -5, 0])
    if k % 512:
        return np.exp2(np.random.permutation(np.resize(levels, k // 32))).repeat(32)
    a = np.empty((k // 512, 16))
    for p in range(k // 512):
        a[p, :8] = np.random.permutation(np.resize(levels, 8))
        for g in range(8):
            far = levels[np.abs(levels - a[p, g]) >= 10]
            a[p, g + 8] = far[np.random.randint(len(far))]
    return np.exp2(a.ravel()).repeat(32)


def f64(x):
    return np.asarray(x).astype(np.float64)


def striped(idx):
    return np.tile(idx.reshape(-1, 16).T, (8, 1)).astype(np.uint16)


def unstriped(offs):
    return offs[:16].T.reshape(-1).astype(np.int64)


def striped8(idx):
    return np.concatenate([x.reshape(-1, 16).T for x in idx]).astype(np.uint16)


def runs(offs, k):
    lists = np.stack([offs[16 * r : 16 * r + 16].T.reshape(-1) for r in range(8)]).astype(np.int64)
    return lists[np.arange(k) % 512 // 64]


def pack_weight(w):
    k, n = w.shape
    w = f64(np.asarray(w, np.float32).astype(ml_dtypes.bfloat16)).reshape(k // 32, 32, n)
    amax = np.abs(w).max(1)
    byte = np.clip(np.where(amax > 0, np.frexp(amax)[1] - 1 + 127 - 7, 1), 1, 254)
    scaled = (w * np.exp2(127.0 - byte)[:, None, :]).reshape(k, n).astype(np.float32)
    words = np.ascontiguousarray(scaled.reshape(k // 512, 128, 4, n).transpose(0, 1, 3, 2)).astype(ml_dtypes.float8_e4m3fn).view(np.uint8)
    return words, np.ascontiguousarray(byte.astype(np.uint8).reshape(k // 512, 16, n))


def unpack_weight(words, scales):
    g, p, n, _ = words.shape
    vals = np.ascontiguousarray(words).view(ml_dtypes.float8_e4m3fn).astype(np.float64) * np.repeat(np.exp2(scales.astype(np.float64) - 127.0), 8, axis=1)[..., None]
    return vals.transpose(0, 1, 3, 2).reshape(g * 512, n)

def planes(y):
    n, m = y.shape
    v = y.astype(np.float32).astype(ml_dtypes.bfloat16).astype(np.float64).reshape(n // 32, 32, m)
    top = np.abs(v).max(1)
    byte = np.clip(np.where(top > 0, np.frexp(top)[1] - 1 + 127 - 7, 1), 1, 254)
    codes = (v * np.exp2(127.0 - byte)[:, None, :]).reshape(n, m).astype(np.float32).astype(ml_dtypes.float8_e4m3fn).view(np.uint8)
    words = codes.reshape(n // 512, 128, 4, m).transpose(0, 1, 3, 2)
    return np.ascontiguousarray(words), np.ascontiguousarray(byte.astype(np.uint8).reshape(n // 512, 16, m))


K, T, S, V, H = 512, 2048, 512, 256, 512


def setup_inputs():
    n = np.random.standard_normal
    s = mx_kscale(K)[:, None]
    u = mx_kscale(S)
    packed_xT = pack_weight(n((K, T)) * s)
    packed_w1 = pack_weight(n((K, H)) / np.sqrt(K) / s)
    packed_w2 = pack_weight(n((K, H)) / np.sqrt(K) / s)
    return {
        "x_words": packed_xT[0],
        "x_scales": packed_xT[1],
        "w1_words": packed_w1[0],
        "w1_scales": packed_w1[1],
        "w2_words": packed_w2[0],
        "w2_scales": packed_w2[1],
        "ga": (np.random.uniform(0.5, 1.5, (H, 1)) * u[:, None]).astype(np.float32),
        "gb": (np.random.uniform(0.5, 1.5, (H, 1)) / u[:, None]).astype(np.float32),
        "offs": striped8(np.random.randint(0, T, (8, S))),
        "two": striped(np.random.permutation(T)[:V]),
        "n1": striped8(np.stack([np.random.permutation(S) for _ in range(8)])),
        "n2": striped8(np.stack([np.random.permutation(S) for _ in range(8)])),
        "n3": striped(np.random.permutation(V)),
        "n4": striped(np.random.permutation(V)),
        "n5": striped8(np.stack([np.random.permutation(V) for _ in range(8)])),
        "n6": striped8(np.stack([np.random.permutation(V) for _ in range(8)])),
    }


def reference(x_words, x_scales, w1_words, w1_scales, w2_words, w2_scales, ga, gb, offs, two, n1, n2, n3, n4, n5, n6):
    xq = unpack_weight(x_words, x_scales)[np.arange(K)[:, None], runs(offs, K)]
    a = unpack_weight(w1_words, w1_scales).T @ xq
    st = np.maximum(a, a[np.arange(H)[:, None], runs(n1, H)])
    z = f64(ga) * (np.minimum(st, st[np.arange(H)[:, None], runs(n2, H)]))
    x_two = unpack_weight(x_words, x_scales)[:, unstriped(two)]
    b = unpack_weight(w2_words, w2_scales).T @ x_two
    z2 = f64(gb) * ((b * b[:, unstriped(n3)]) * (np.tanh(b[:, unstriped(n4)])))
    s = 0.0625 * ((mxq(z, 0, "e4m3").T @ mxq(z2, 0, "e4m3")))
    ex = np.exp(s)
    out_0 = np.log(ex + ex[np.arange(S)[:, None], runs(n5, S)]) - (s[np.arange(S)[:, None], runs(n6, S)])
    return (out_0,) + planes(out_0)

@@ -1,0 +1,262 @@
+from contextlib import ExitStack
+
+import concourse.mybir as mybir
+from concourse.masks import make_identity
+
+F32 = mybir.dt.float32
+BF16 = mybir.dt.bfloat16
+I32 = mybir.dt.int32
+U32 = mybir.dt.uint32
+U16 = mybir.dt.uint16
+U8 = mybir.dt.uint8
+FP8X4 = mybir.dt.float8_e4m3fn_x4
+ALU = mybir.AluOpType
+ACT = mybir.ActivationFunctionType
+
+P = 128
+T = 2048
+S = 512
+V = 256
+H = 512
+PLANES = 4
+V_WINDOW = V + 16
+FLOPS = 2 * 512 * H * S + 2 * 512 * H * V + 2 * H * S * V
+
+
+def tile_picked_hkqhopmncubelse_none_po_kernel(
+    tc, x_words, x_scales, w1_words, w1_scales, w2_words, w2_scales, ga, gb,
+    offs, two, n1, n2, n3, n4, n5, n6, out_0, out_1, out_2,
+):
+    nc = tc.nc
+    with ExitStack() as ctx:
+        pool = ctx.enter_context(tc.tile_pool(name="pool", bufs=1))
+        psum = ctx.enter_context(tc.psum_pool(name="psum", bufs=1))
+
+        def sb(name, shape, dtype):
+            return pool.tile(shape, dtype, name=name, align_bytes=64)
+
+        def load_list(name, src):
+            t = sb(name, list(src.shape), U16)
+            nc.sync.dma_start(t[:], src)
+            return t
+
+        def words_of(src):
+            return src[0].rearrange("p n t -> p (n t)").bitcast(I32)
+
+        xs_win = sb("xs_win", [P, T], U8)
+        nc.vector.memset(xs_win[:].bitcast(I32), 0)
+        ws_raw = sb("ws_raw", [P, 2, H // 4], I32)
+        nc.gpsimd.memset(ws_raw[:], 0)
+        two_l = load_list("two_l", two)
+        offs_l = load_list("offs_l", offs)
+        n3_l = load_list("n3_l", n3)
+        n4_l = load_list("n4_l", n4)
+        n1_l = load_list("n1_l", n1)
+        xw_win = sb("xw_win", [P, T], U32)
+        nc.sync.dma_start(xw_win[:].bitcast(I32), words_of(x_words))
+        w2_raw = sb("w2_raw", [P, H], I32)
+        nc.sync.dma_start(w2_raw[:], words_of(w2_words))
+        w1_raw = sb("w1_raw", [P, H], I32)
+        nc.sync.dma_start(w1_raw[:], words_of(w1_words))
+        nc.scalar.dma_start(xs_win[0:P:8, :].bitcast(I32), x_scales[0].bitcast(I32))
+        nc.scalar.dma_start(ws_raw[0:P:8, 0, :], w2_scales[0].bitcast(I32))
+        nc.scalar.dma_start(ws_raw[0:P:8, 1, :], w1_scales[0].bitcast(I32))
+        n2_l = load_list("n2_l", n2)
+        n5_l = load_list("n5_l", n5)
+        n6_l = load_list("n6_l", n6)
+
+        g_rows = sb("g_rows", [P, P], F32)
+        nc.gpsimd.memset(g_rows[:], 0.0)
+        for i, g in enumerate((ga, gb)):
+            nc.gpsimd.dma_start(
+                g_rows[4 * i : 4 * i + 4, :].rearrange("t (a b) -> t a b", b=8),
+                g.rearrange("(a t b) o -> t a (b o)", t=PLANES, b=8),
+            )
+        ident = sb("ident", [P, P], F32)
+        make_identity(nc, ident[:])
+
+        xs_got = sb("xs_got", [P, V + S], U8)
+        nc.vector.tensor_copy(xs_got[:, :V], xs_win[:].indirect(two_l[:]))
+        nc.vector.tensor_copy(xs_got[:, V:], xs_win[:].indirect(offs_l[:]))
+        planes = sb("planes", [P, V + S + 2 * H], U8)
+        x_plane = planes[:, : V + S]
+        w_plane = planes[:, V + S :]
+        nc.vector.tensor_copy(
+            w_plane.bitcast(I32).rearrange("p (w t a b) -> p w a t b", w=2, t=PLANES, b=2),
+            ws_raw[:].rearrange("p w (a t b) -> p w a t b", t=PLANES, b=2),
+        )
+        nc.vector.tensor_copy(x_plane.bitcast(I32), xs_got[:].bitcast(I32))
+        for i in range(1, 4):
+            nc.scalar.dma_start(planes[i:P:32, :].bitcast(I32), planes[8 * i : P : 32, :].bitcast(I32))
+
+        g_ps = psum.tile([P, P], F32, name="g_ps", tag="a3")
+        nc.tensor.transpose(g_ps[:], g_rows[:], ident[:])
+        ga_abs = sb("ga_abs", [P, PLANES], F32)
+        ga_sign = sb("ga_sign", [P, PLANES], F32)
+        gb_signed = sb("gb_signed", [P, PLANES], F32)
+        nc.scalar.activation(ga_abs[:], g_ps[:, 0:4], ACT.Abs)
+        nc.scalar.activation(ga_sign[:], g_ps[:, 0:4], ACT.Sign)
+        nc.vector.tensor_tensor(gb_signed[:], g_ps[:, 4:8], ga_sign[:], ALU.mult)
+
+        def deal(name, raw):
+            dealt = sb(name, [P, H], U32)
+            nc.vector.tensor_copy(
+                dealt[:].bitcast(I32).rearrange("p (t a b) -> p a t b", t=PLANES, b=8),
+                raw[:].rearrange("p (a t b) -> p a t b", t=PLANES, b=8),
+            )
+            return dealt
+
+        w2_codes = deal("w2_codes", w2_raw)
+        x_two = sb("x_two", [P, V], U32)
+        nc.vector.tensor_copy(x_two[:], xw_win[:].indirect(two_l[:]))
+        b_ps = []
+        for t in range(PLANES):
+            ps = psum.tile([P, V], F32, name=f"b_ps{t}", tag=f"b{t}")
+            nc.tensor.matmul_mx(
+                out=ps[:], lhsT=w2_codes[:, t * P : (t + 1) * P].bitcast(FP8X4), lhsT_scale=w_plane[:, t * P : (t + 1) * P],
+                rhs=x_two[:].bitcast(FP8X4), rhs_scale=x_plane[:, :V], start=True, stop=True,
+            )
+            b_ps.append(ps)
+        w1_codes = deal("w1_codes", w1_raw)
+        x_offs = sb("x_offs", [P, S], U32)
+        nc.vector.tensor_copy(x_offs[:], xw_win[:].indirect(offs_l[:]))
+        a_ps = []
+        for t in range(PLANES):
+            ps = psum.tile([P, S], F32, name=f"a_ps{t}", tag=f"a{t}")
+            nc.tensor.matmul_mx(
+                out=ps[:], lhsT=w1_codes[:, t * P : (t + 1) * P].bitcast(FP8X4), lhsT_scale=w_plane[:, H + t * P : H + (t + 1) * P],
+                rhs=x_offs[:].bitcast(FP8X4), rhs_scale=x_plane[:, V:], start=True, stop=True,
+            )
+            a_ps.append(ps)
+
+        z2_f = sb("z2_f", [P, PLANES, V], F32)
+        z_pl = sb("z_pl", [P, PLANES, S], BF16)
+
+        def b_scalar(t):
+            b_win = sb(f"b_win{t}", [P, V_WINDOW], F32)
+            nc.scalar.activation(b_win[:, :V], b_ps[t][:], ACT.Copy, scale=gb_signed[:, t : t + 1])
+            tanh_win = sb(f"tanh_win{t}", [P, V_WINDOW], F32)
+            nc.scalar.activation(tanh_win[:, :V], b_ps[t][:], ACT.Tanh)
+            b3 = sb(f"b3_{t}", [P, V], F32)
+            nc.scalar.activation(b3[:], b_win[:].indirect(n3_l[:]), ACT.Copy)
+            return tanh_win, b3
+
+        def b_vector(t, tanh_win, b3):
+            bb = sb(f"bb{t}", [P, V], F32)
+            nc.vector.tensor_tensor(bb[:], b_ps[t][:], b3[:], ALU.mult)
+            nc.vector.tensor_tensor(z2_f[:, t, :], tanh_win[:].indirect(n4_l[:]), bb[:], ALU.mult)
+
+        def a_out(t):
+            a_win = sb(f"a_win{t}", [P, 2 * S], F32)
+            nc.vector.tensor_scalar(a_win[:, :S], a_ps[t][:], ga_abs[:, t : t + 1], None, ALU.mult)
+            a1 = sb(f"a1_{t}", [P, S], F32)
+            nc.scalar.activation(a1[:], a_win[:].indirect(n1_l[:]), ACT.Copy)
+            return a_win, a1
+
+        def a_max(t, a_win, a1):
+            st_win = sb(f"st_win{t}", [P, 2 * S], F32)
+            nc.vector.tensor_tensor(st_win[:, :S], a_win[:, :S], a1[:], ALU.max)
+            return st_win
+
+        def a_fetch(t, st_win):
+            st2 = sb(f"st2_{t}", [P, S], F32)
+            if t == PLANES - 1:
+                nc.vector.tensor_copy(st2[:], st_win[:].indirect(n2_l[:]))
+            else:
+                nc.scalar.activation(st2[:], st_win[:].indirect(n2_l[:]), ACT.Copy)
+            return st2
+
+        def a_min(t, st_win, st2):
+            nc.vector.tensor_tensor(
+                z_pl[:, t, :].rearrange("p (u m) -> p m u", u=PLANES),
+                st_win[:, :S].rearrange("p (m u) -> p m u", u=PLANES),
+                st2[:].rearrange("p (m u) -> p m u", u=PLANES),
+                ALU.min,
+            )
+
+        bs = {}
+        for t in (0, 1):
+            bs[t] = b_scalar(t)
+        b_vector(0, *bs[0])
+        aw = [a_out(t) for t in range(PLANES)]
+        b_vector(1, *bs[1])
+        st = [a_max(t, *aw[t]) for t in range(PLANES)]
+        for t in (2, 3):
+            bs[t] = b_scalar(t)
+        st2s = [a_fetch(t, st[t]) for t in range(PLANES)]
+        for t in (2, 3):
+            b_vector(t, *bs[t])
+        z2_bf = sb("z2_bf", [P, V * PLANES], BF16)
+        nc.vector.tensor_copy(
+            z2_bf[:].rearrange("p (c i t) -> p c t i", i=4, t=PLANES),
+            z2_f[:].rearrange("p t (c i) -> p c t i", i=4),
+        )
+        z2_codes = sb("z2_codes", [P, V], U32)
+        z2_plane = sb("z2_plane", [P, V], U8)
+        a_min(0, st[0], st2s[0])
+        nc.vector.quantize_mx(out=z2_codes[:].bitcast(FP8X4), scales=z2_plane[:], in_=z2_bf[:])
+        for t in range(1, PLANES):
+            a_min(t, st[t], st2s[t])
+
+        total = sb("total", [P, PLANES, V], F32)
+        s_wins = []
+        z_bfs = []
+        for u in range(PLANES):
+            z_bf = sb(f"z_bf{u}", [P, P * PLANES], BF16)
+            z_bfs.append(z_bf)
+
+        def weave(u):
+            nc.vector.tensor_copy(
+                z_bfs[u][:].rearrange("p (c i t) -> p c t i", i=4, t=PLANES),
+                z_pl[:, :, u * P : (u + 1) * P].rearrange("p t (c i) -> p c t i", i=4),
+            )
+
+        def scores(u):
+            z_codes = sb(f"z_codes{u}", [P, P], U32)
+            z_plane = sb(f"z_plane{u}", [P, P], U8)
+            nc.vector.quantize_mx(out=z_codes[:].bitcast(FP8X4), scales=z_plane[:], in_=z_bfs[u][:])
+            ps = psum.tile([P, V], F32, name=f"s_ps{u}", tag=f"b{u}")
+            nc.tensor.matmul_mx(
+                out=ps[:], lhsT=z_codes[:].bitcast(FP8X4), lhsT_scale=z_plane[:],
+                rhs=z2_codes[:].bitcast(FP8X4), rhs_scale=z2_plane[:], start=True, stop=True,
+            )
+            ex_win = sb(f"ex_win{u}", [P, 2 * V], F32)
+            nc.scalar.activation(ex_win[:, :V], ps[:], ACT.Exp, scale=0.0625)
+            return ps, ex_win
+
+        weave(0)
+        sc = []
+        for u in range(PLANES):
+            if u + 1 < PLANES:
+                weave(u + 1)
+            sc.append(scores(u))
+        ex5s = []
+        for u in range(PLANES):
+            ps, ex_win = sc[u]
+            s_win = sb(f"s_win{u}", [P, 2 * V], F32)
+            nc.vector.tensor_scalar(s_win[:, :V], ps[:], 0.0625, None, ALU.mult)
+            s_wins.append(s_win)
+            ex5 = sb(f"ex5_{u}", [P, V], F32)
+            nc.scalar.activation(ex5[:], ex_win[:].indirect(n5_l[:]), ACT.Copy)
+            ex5s.append(ex5)
+        for u in range(PLANES):
+            nc.vector.tensor_tensor(total[:, u, :], sc[u][1][:, :V], ex5s[u][:], ALU.add)
+        log_total = sb("log_total", [P, PLANES, V], F32)
+        nc.scalar.activation(log_total[:], total[:], ACT.Ln)
+        out_rows = out_0.rearrange("(p u) v -> p u v", u=PLANES)
+        result = sb("result", [P, PLANES, V], F32)
+        out_bf = sb("out_bf", [P, V, PLANES], BF16)
+        for u in range(PLANES):
+            s6 = total[:, u, :]
+            nc.scalar.activation(s6, s_wins[u][:].indirect(n6_l[:]), ACT.Copy)
+            nc.vector.tensor_tensor(result[:, u, :], log_total[:, u, :], s6, ALU.subtract)
+            nc.sync.dma_start(out_rows[:, u, :], result[:, u, :])
+            if u % 2 == 1:
+                nc.vector.tensor_copy(out_bf[:, :, u - 1 : u + 1], result[:, u - 1 : u + 1, :].rearrange("p u v -> p v u"))
+        out_codes = sb("out_codes", [P, V], U32)
+        out_plane = sb("out_plane", [P, V], U8)
+        nc.vector.quantize_mx(out=out_codes[:].bitcast(FP8X4), scales=out_plane[:], in_=out_bf[:].rearrange("p v u -> p (v u)"))
+        nc.sync.dma_start(words_of(out_1), out_codes[:].bitcast(I32))
+        for q in range(4):
+            queue = nc.sync if q % 2 == 0 else nc.scalar
+            queue.dma_start(out_2[0, 4 * q : 4 * q + 4, :].bitcast(I32), out_plane[32 * q : 32 * q + 4, :].bitcast(I32))

@@ -44,20 +44,24 @@ def tile_picked_hkqhopmncubelse_none_po_kernel(
             return src[0].rearrange("p n t -> p (n t)").bitcast(I32)
 
         xs_win = sb("xs_win", [P, T], U8)
-        nc.vector.memset(xs_win[:].bitcast(I32), 0)
+        nc.gpsimd.memset(xs_win[:, : T // 2].bitcast(I32), 0)
+        nc.vector.memset(xs_win[:, T // 2 :].bitcast(I32), 0)
         ws_raw = sb("ws_raw", [P, 2, H // 4], I32)
-        nc.gpsimd.memset(ws_raw[:], 0)
+        nc.vector.memset(ws_raw[:], 0)
         two_l = load_list("two_l", two)
         offs_l = load_list("offs_l", offs)
-        n3_l = load_list("n3_l", n3)
-        n4_l = load_list("n4_l", n4)
+        g_raw = sb("g_raw", [2, H], F32)
+        for i, g in enumerate((ga, gb)):
+            nc.sync.dma_start(g_raw[i : i + 1, :], g.rearrange("h o -> o h"))
         n1_l = load_list("n1_l", n1)
         xw_win = sb("xw_win", [P, T], U32)
         nc.sync.dma_start(xw_win[:].bitcast(I32), words_of(x_words))
-        w2_raw = sb("w2_raw", [P, H], I32)
-        nc.sync.dma_start(w2_raw[:], words_of(w2_words))
+        n3_l = load_list("n3_l", n3)
+        n4_l = load_list("n4_l", n4)
         w1_raw = sb("w1_raw", [P, H], I32)
         nc.sync.dma_start(w1_raw[:], words_of(w1_words))
+        w2_raw = sb("w2_raw", [P, H], I32)
+        nc.sync.dma_start(w2_raw[:], words_of(w2_words))
         nc.scalar.dma_start(xs_win[0:P:8, :].bitcast(I32), x_scales[0].bitcast(I32))
         nc.scalar.dma_start(ws_raw[0:P:8, 0, :], w2_scales[0].bitcast(I32))
         nc.scalar.dma_start(ws_raw[0:P:8, 1, :], w1_scales[0].bitcast(I32))
@@ -65,15 +69,14 @@ def tile_picked_hkqhopmncubelse_none_po_kernel(
         n5_l = load_list("n5_l", n5)
         n6_l = load_list("n6_l", n6)
 
-        g_rows = sb("g_rows", [P, P], F32)
-        nc.gpsimd.memset(g_rows[:], 0.0)
-        for i, g in enumerate((ga, gb)):
-            nc.gpsimd.dma_start(
-                g_rows[4 * i : 4 * i + 4, :].rearrange("t (a b) -> t a b", b=8),
-                g.rearrange("(a t b) o -> t a (b o)", t=PLANES, b=8),
-            )
+        g_rows = sb("g_rows", [P, H], F32)
+        nc.vector.memset(g_rows[:], 0.0)
         ident = sb("ident", [P, P], F32)
         make_identity(nc, ident[:])
+        nc.vector.tensor_copy(
+            g_rows[0:2, :].rearrange("p (t a b) -> p a t b", t=PLANES, b=8),
+            g_raw[:].rearrange("p (a t b) -> p a t b", t=PLANES, b=8),
+        )
 
         xs_got = sb("xs_got", [P, V + S], U8)
         nc.vector.tensor_copy(xs_got[:, :V], xs_win[:].indirect(two_l[:]))
@@ -89,14 +92,15 @@ def tile_picked_hkqhopmncubelse_none_po_kernel(
         for i in range(1, 4):
             nc.scalar.dma_start(planes[i:P:32, :].bitcast(I32), planes[8 * i : P : 32, :].bitcast(I32))
 
-        g_ps = psum.tile([P, P], F32, name="g_ps", tag="a3")
-        nc.tensor.transpose(g_ps[:], g_rows[:], ident[:])
+        g_ps = psum.tile([P, PLANES, P], F32, name="g_ps", tag="a0")
+        for t in range(PLANES):
+            nc.tensor.transpose(g_ps[:, t, :], g_rows[:, t * P : (t + 1) * P], ident[:])
         ga_abs = sb("ga_abs", [P, PLANES], F32)
         ga_sign = sb("ga_sign", [P, PLANES], F32)
         gb_signed = sb("gb_signed", [P, PLANES], F32)
-        nc.scalar.activation(ga_abs[:], g_ps[:, 0:4], ACT.Abs)
-        nc.scalar.activation(ga_sign[:], g_ps[:, 0:4], ACT.Sign)
-        nc.vector.tensor_tensor(gb_signed[:], g_ps[:, 4:8], ga_sign[:], ALU.mult)
+        nc.scalar.activation(ga_abs[:], g_ps[:, :, 0], ACT.Abs)
+        nc.scalar.activation(ga_sign[:], g_ps[:, :, 0], ACT.Sign)
+        nc.vector.tensor_tensor(gb_signed[:], g_ps[:, :, 1], ga_sign[:], ALU.mult)
 
         def deal(name, raw):
             dealt = sb(name, [P, H], U32)
@@ -106,17 +110,6 @@ def tile_picked_hkqhopmncubelse_none_po_kernel(
             )
             return dealt
 
-        w2_codes = deal("w2_codes", w2_raw)
-        x_two = sb("x_two", [P, V], U32)
-        nc.vector.tensor_copy(x_two[:], xw_win[:].indirect(two_l[:]))
-        b_ps = []
-        for t in range(PLANES):
-            ps = psum.tile([P, V], F32, name=f"b_ps{t}", tag=f"b{t}")
-            nc.tensor.matmul_mx(
-                out=ps[:], lhsT=w2_codes[:, t * P : (t + 1) * P].bitcast(FP8X4), lhsT_scale=w_plane[:, t * P : (t + 1) * P],
-                rhs=x_two[:].bitcast(FP8X4), rhs_scale=x_plane[:, :V], start=True, stop=True,
-            )
-            b_ps.append(ps)
         w1_codes = deal("w1_codes", w1_raw)
         x_offs = sb("x_offs", [P, S], U32)
         nc.vector.tensor_copy(x_offs[:], xw_win[:].indirect(offs_l[:]))
@@ -128,11 +121,22 @@ def tile_picked_hkqhopmncubelse_none_po_kernel(
                 rhs=x_offs[:].bitcast(FP8X4), rhs_scale=x_plane[:, V:], start=True, stop=True,
             )
             a_ps.append(ps)
+        w2_codes = deal("w2_codes", w2_raw)
+        x_two = sb("x_two", [P, V], U32)
+        nc.vector.tensor_copy(x_two[:], xw_win[:].indirect(two_l[:]))
+        b_ps = []
+        for t in range(PLANES):
+            ps = psum.tile([P, V], F32, name=f"b_ps{t}", tag=f"b{t}")
+            nc.tensor.matmul_mx(
+                out=ps[:], lhsT=w2_codes[:, t * P : (t + 1) * P].bitcast(FP8X4), lhsT_scale=w_plane[:, t * P : (t + 1) * P],
+                rhs=x_two[:].bitcast(FP8X4), rhs_scale=x_plane[:, :V], start=True, stop=True,
+            )
+            b_ps.append(ps)
 
         z2_f = sb("z2_f", [P, PLANES, V], F32)
         z_pl = sb("z_pl", [P, PLANES, S], BF16)
 
-        def b_scalar(t):
+        def b_fetch(t):
             b_win = sb(f"b_win{t}", [P, V_WINDOW], F32)
             nc.scalar.activation(b_win[:, :V], b_ps[t][:], ACT.Copy, scale=gb_signed[:, t : t + 1])
             tanh_win = sb(f"tanh_win{t}", [P, V_WINDOW], F32)
@@ -141,14 +145,17 @@ def tile_picked_hkqhopmncubelse_none_po_kernel(
             nc.scalar.activation(b3[:], b_win[:].indirect(n3_l[:]), ACT.Copy)
             return tanh_win, b3
 
-        def b_vector(t, tanh_win, b3):
+        def b_product(t, tanh_win, b3):
             bb = sb(f"bb{t}", [P, V], F32)
             nc.vector.tensor_tensor(bb[:], b_ps[t][:], b3[:], ALU.mult)
             nc.vector.tensor_tensor(z2_f[:, t, :], tanh_win[:].indirect(n4_l[:]), bb[:], ALU.mult)
 
-        def a_out(t):
+        def a_fetch(t):
             a_win = sb(f"a_win{t}", [P, 2 * S], F32)
-            nc.vector.tensor_scalar(a_win[:, :S], a_ps[t][:], ga_abs[:, t : t + 1], None, ALU.mult)
+            if t < 2:
+                nc.scalar.activation(a_win[:, :S], a_ps[t][:], ACT.Copy, scale=ga_abs[:, t : t + 1])
+            else:
+                nc.vector.tensor_scalar(a_win[:, :S], a_ps[t][:], ga_abs[:, t : t + 1], None, ALU.mult)
             a1 = sb(f"a1_{t}", [P, S], F32)
             nc.scalar.activation(a1[:], a_win[:].indirect(n1_l[:]), ACT.Copy)
             return a_win, a1
@@ -158,15 +165,15 @@ def tile_picked_hkqhopmncubelse_none_po_kernel(
             nc.vector.tensor_tensor(st_win[:, :S], a_win[:, :S], a1[:], ALU.max)
             return st_win
 
-        def a_fetch(t, st_win):
+        def st_fetch(t, st_win):
             st2 = sb(f"st2_{t}", [P, S], F32)
-            if t == PLANES - 1:
+            if t < 2:
                 nc.vector.tensor_copy(st2[:], st_win[:].indirect(n2_l[:]))
             else:
                 nc.scalar.activation(st2[:], st_win[:].indirect(n2_l[:]), ACT.Copy)
             return st2
 
-        def a_min(t, st_win, st2):
+        def st_min(t, st_win, st2):
             nc.vector.tensor_tensor(
                 z_pl[:, t, :].rearrange("p (u m) -> p m u", u=PLANES),
                 st_win[:, :S].rearrange("p (m u) -> p m u", u=PLANES),
@@ -174,29 +181,38 @@ def tile_picked_hkqhopmncubelse_none_po_kernel(
                 ALU.min,
             )
 
-        bs = {}
-        for t in (0, 1):
-            bs[t] = b_scalar(t)
-        b_vector(0, *bs[0])
-        aw = [a_out(t) for t in range(PLANES)]
-        b_vector(1, *bs[1])
-        st = [a_max(t, *aw[t]) for t in range(PLANES)]
-        for t in (2, 3):
-            bs[t] = b_scalar(t)
-        st2s = [a_fetch(t, st[t]) for t in range(PLANES)]
-        for t in (2, 3):
-            b_vector(t, *bs[t])
+        a_got, b_got, st, st2 = {}, {}, {}, {}
+        a_got[0] = a_fetch(0)
+        b_got[0] = b_fetch(0)
+        for t in (1, 2):
+            a_got[t] = a_fetch(t)
+            b_product(t - 1, *b_got[t - 1])
+            st[t - 1] = a_max(t - 1, *a_got[t - 1])
+            if t == 1:
+                b_got[1] = b_fetch(1)
+        a_got[3] = a_fetch(3)
+        b_got[2] = b_fetch(2)
+        st[2] = a_max(2, *a_got[2])
+        b_product(2, *b_got[2])
+        st[3] = a_max(3, *a_got[3])
+        b_got[3] = b_fetch(3)
+        st2[0] = st_fetch(0, st[0])
+        b_product(3, *b_got[3])
+        st2[1] = st_fetch(1, st[1])
+        st_min(0, st[0], st2[0])
+        st2[2] = st_fetch(2, st[2])
         z2_bf = sb("z2_bf", [P, V * PLANES], BF16)
-        nc.vector.tensor_copy(
+        nc.scalar.copy(
             z2_bf[:].rearrange("p (c i t) -> p c t i", i=4, t=PLANES),
             z2_f[:].rearrange("p t (c i) -> p c t i", i=4),
         )
+        st_min(1, st[1], st2[1])
+        st2[3] = st_fetch(3, st[3])
         z2_codes = sb("z2_codes", [P, V], U32)
         z2_plane = sb("z2_plane", [P, V], U8)
-        a_min(0, st[0], st2s[0])
         nc.vector.quantize_mx(out=z2_codes[:].bitcast(FP8X4), scales=z2_plane[:], in_=z2_bf[:])
-        for t in range(1, PLANES):
-            a_min(t, st[t], st2s[t])
+        st_min(2, st[2], st2[2])
+        st_min(3, st[3], st2[3])
 
         total = sb("total", [P, PLANES, V], F32)
         s_wins = []
@@ -206,7 +222,8 @@ def tile_picked_hkqhopmncubelse_none_po_kernel(
             z_bfs.append(z_bf)
 
         def weave(u):
-            nc.vector.tensor_copy(
+            copy = nc.scalar.copy if u == 1 else nc.vector.tensor_copy
+            copy(
                 z_bfs[u][:].rearrange("p (c i t) -> p c t i", i=4, t=PLANES),
                 z_pl[:, :, u * P : (u + 1) * P].rearrange("p t (c i) -> p c t i", i=4),
             )
@@ -222,40 +239,51 @@ def tile_picked_hkqhopmncubelse_none_po_kernel(
             )
             ex_win = sb(f"ex_win{u}", [P, 2 * V], F32)
             nc.scalar.activation(ex_win[:, :V], ps[:], ACT.Exp, scale=0.0625)
-            return ps, ex_win
-
-        weave(0)
-        sc = []
-        for u in range(PLANES):
-            if u + 1 < PLANES:
-                weave(u + 1)
-            sc.append(scores(u))
-        ex5s = []
-        for u in range(PLANES):
-            ps, ex_win = sc[u]
-            s_win = sb(f"s_win{u}", [P, 2 * V], F32)
-            nc.vector.tensor_scalar(s_win[:, :V], ps[:], 0.0625, None, ALU.mult)
-            s_wins.append(s_win)
             ex5 = sb(f"ex5_{u}", [P, V], F32)
             nc.scalar.activation(ex5[:], ex_win[:].indirect(n5_l[:]), ACT.Copy)
-            ex5s.append(ex5)
+            return ps, ex_win, ex5
+
+        sc = []
+        for pair in (0, 2):
+            weave(pair)
+            weave(pair + 1)
+            sc.append(scores(pair))
+            sc.append(scores(pair + 1))
         for u in range(PLANES):
-            nc.vector.tensor_tensor(total[:, u, :], sc[u][1][:, :V], ex5s[u][:], ALU.add)
+            s_win = sb(f"s_win{u}", [P, 2 * V], F32)
+            nc.vector.tensor_scalar(s_win[:, :V], sc[u][0][:], 0.0625, None, ALU.mult)
+            s_wins.append(s_win)
+        for u in range(PLANES):
+            nc.vector.tensor_tensor(total[:, u, :], sc[u][1][:, :V], sc[u][2][:], ALU.add)
         log_total = sb("log_total", [P, PLANES, V], F32)
         nc.scalar.activation(log_total[:], total[:], ACT.Ln)
         out_rows = out_0.rearrange("(p u) v -> p u v", u=PLANES)
         result = sb("result", [P, PLANES, V], F32)
         out_bf = sb("out_bf", [P, V, PLANES], BF16)
-        for u in range(PLANES):
-            s6 = total[:, u, :]
-            nc.scalar.activation(s6, s_wins[u][:].indirect(n6_l[:]), ACT.Copy)
-            nc.vector.tensor_tensor(result[:, u, :], log_total[:, u, :], s6, ALU.subtract)
-            nc.sync.dma_start(out_rows[:, u, :], result[:, u, :])
-            if u % 2 == 1:
-                nc.vector.tensor_copy(out_bf[:, :, u - 1 : u + 1], result[:, u - 1 : u + 1, :].rearrange("p u v -> p v u"))
         out_codes = sb("out_codes", [P, V], U32)
         out_plane = sb("out_plane", [P, V], U8)
-        nc.vector.quantize_mx(out=out_codes[:].bitcast(FP8X4), scales=out_plane[:], in_=out_bf[:].rearrange("p v u -> p (v u)"))
+
+        def finish(u, cols):
+            s6 = sc[PLANES - 1][2][:, cols] if u == 0 else total[:, u, cols]
+            nc.scalar.activation(s6, s_wins[u][:].indirect(n6_l[:, cols.start // 16 : cols.stop // 16]), ACT.Copy)
+            nc.vector.tensor_tensor(result[:, u, cols], log_total[:, u, cols], s6, ALU.subtract)
+
+        def round_pair(u, cols):
+            nc.vector.tensor_copy(out_bf[:, cols, u : u + 2], result[:, u : u + 2, cols].rearrange("p u v -> p v u"))
+
+        for u in range(PLANES - 1):
+            finish(u, slice(0, V))
+            nc.sync.dma_start(out_rows[:, u, :], result[:, u, :])
+            if u == 1:
+                round_pair(0, slice(0, V))
+        for cols in (slice(0, V // 2), slice(V // 2, V)):
+            finish(PLANES - 1, cols)
+            round_pair(2, cols)
+            nc.vector.quantize_mx(
+                out=out_codes[:, cols].bitcast(FP8X4), scales=out_plane[:, cols],
+                in_=out_bf[:, cols, :].rearrange("p v u -> p (v u)"),
+            )
+        nc.sync.dma_start(out_rows[:, PLANES - 1, :], result[:, PLANES - 1, :])
         nc.sync.dma_start(words_of(out_1), out_codes[:].bitcast(I32))
         for q in range(4):
             queue = nc.sync if q % 2 == 0 else nc.scalar

@@ -48,23 +48,23 @@ def tile_picked_hkqhopmncubelse_none_po_kernel(
         nc.vector.memset(xs_win[:, T // 2 :].bitcast(I32), 0)
         ws_raw = sb("ws_raw", [P, 2, H // 4], I32)
         nc.vector.memset(ws_raw[:], 0)
-        two_l = load_list("two_l", two)
-        offs_l = load_list("offs_l", offs)
         g_raw = sb("g_raw", [2, H], F32)
         for i, g in enumerate((ga, gb)):
-            nc.sync.dma_start(g_raw[i : i + 1, :], g.rearrange("h o -> o h"))
-        n1_l = load_list("n1_l", n1)
+            nc.scalar.dma_start(g_raw[i : i + 1, :], g.rearrange("h o -> o h"))
+        nc.scalar.dma_start(xs_win[0:P:8, :].bitcast(I32), x_scales[0].bitcast(I32))
+        two_l = load_list("two_l", two)
+        offs_l = load_list("offs_l", offs)
+        nc.sync.dma_start(ws_raw[0:P:8, 1, :], w1_scales[0].bitcast(I32))
+        nc.sync.dma_start(ws_raw[0:P:8, 0, :], w2_scales[0].bitcast(I32))
         xw_win = sb("xw_win", [P, T], U32)
         nc.sync.dma_start(xw_win[:].bitcast(I32), words_of(x_words))
+        n1_l = load_list("n1_l", n1)
         n3_l = load_list("n3_l", n3)
         n4_l = load_list("n4_l", n4)
-        w1_raw = sb("w1_raw", [P, H], I32)
-        nc.sync.dma_start(w1_raw[:], words_of(w1_words))
         w2_raw = sb("w2_raw", [P, H], I32)
         nc.sync.dma_start(w2_raw[:], words_of(w2_words))
-        nc.scalar.dma_start(xs_win[0:P:8, :].bitcast(I32), x_scales[0].bitcast(I32))
-        nc.scalar.dma_start(ws_raw[0:P:8, 0, :], w2_scales[0].bitcast(I32))
-        nc.scalar.dma_start(ws_raw[0:P:8, 1, :], w1_scales[0].bitcast(I32))
+        w1_raw = sb("w1_raw", [P, H], I32)
+        nc.sync.dma_start(w1_raw[:], words_of(w1_words))
         n2_l = load_list("n2_l", n2)
         n5_l = load_list("n5_l", n5)
         n6_l = load_list("n6_l", n6)
@@ -73,7 +73,7 @@ def tile_picked_hkqhopmncubelse_none_po_kernel(
         nc.vector.memset(g_rows[:], 0.0)
         ident = sb("ident", [P, P], F32)
         make_identity(nc, ident[:])
-        nc.vector.tensor_copy(
+        nc.scalar.copy(
             g_rows[0:2, :].rearrange("p (t a b) -> p a t b", t=PLANES, b=8),
             g_raw[:].rearrange("p (a t b) -> p a t b", t=PLANES, b=8),
         )
@@ -84,7 +84,7 @@ def tile_picked_hkqhopmncubelse_none_po_kernel(
         planes = sb("planes", [P, V + S + 2 * H], U8)
         x_plane = planes[:, : V + S]
         w_plane = planes[:, V + S :]
-        nc.vector.tensor_copy(
+        nc.gpsimd.tensor_copy(
             w_plane.bitcast(I32).rearrange("p (w t a b) -> p w a t b", w=2, t=PLANES, b=2),
             ws_raw[:].rearrange("p w (a t b) -> p w a t b", t=PLANES, b=2),
         )
@@ -92,7 +92,7 @@ def tile_picked_hkqhopmncubelse_none_po_kernel(
         for i in range(1, 4):
             nc.scalar.dma_start(planes[i:P:32, :].bitcast(I32), planes[8 * i : P : 32, :].bitcast(I32))
 
-        g_ps = psum.tile([P, PLANES, P], F32, name="g_ps", tag="a0")
+        g_ps = psum.tile([P, PLANES, P], F32, name="g_ps", tag="b0")
         for t in range(PLANES):
             nc.tensor.transpose(g_ps[:, t, :], g_rows[:, t * P : (t + 1) * P], ident[:])
         ga_abs = sb("ga_abs", [P, PLANES], F32)
@@ -100,7 +100,9 @@ def tile_picked_hkqhopmncubelse_none_po_kernel(
         gb_signed = sb("gb_signed", [P, PLANES], F32)
         nc.scalar.activation(ga_abs[:], g_ps[:, :, 0], ACT.Abs)
         nc.scalar.activation(ga_sign[:], g_ps[:, :, 0], ACT.Sign)
-        nc.vector.tensor_tensor(gb_signed[:], g_ps[:, :, 1], ga_sign[:], ALU.mult)
+        gb_dealt = sb("gb_dealt", [P, PLANES], F32)
+        nc.scalar.copy(gb_dealt[:], g_ps[:, :, 1])
+        nc.gpsimd.tensor_tensor(gb_signed[:], gb_dealt[:], ga_sign[:], ALU.mult)
 
         def deal(name, raw):
             dealt = sb(name, [P, H], U32)
@@ -110,28 +112,32 @@ def tile_picked_hkqhopmncubelse_none_po_kernel(
             )
             return dealt
 
-        w1_codes = deal("w1_codes", w1_raw)
+        x_two = sb("x_two", [P, V], U32)
+        nc.vector.tensor_copy(x_two[:], xw_win[:].indirect(two_l[:]))
+        w2_codes = deal("w2_codes", w2_raw)
         x_offs = sb("x_offs", [P, S], U32)
         nc.vector.tensor_copy(x_offs[:], xw_win[:].indirect(offs_l[:]))
-        a_ps = []
-        for t in range(PLANES):
+        w1_codes = deal("w1_codes", w1_raw)
+
+        def project_a(t):
             ps = psum.tile([P, S], F32, name=f"a_ps{t}", tag=f"a{t}")
             nc.tensor.matmul_mx(
                 out=ps[:], lhsT=w1_codes[:, t * P : (t + 1) * P].bitcast(FP8X4), lhsT_scale=w_plane[:, H + t * P : H + (t + 1) * P],
                 rhs=x_offs[:].bitcast(FP8X4), rhs_scale=x_plane[:, V:], start=True, stop=True,
             )
-            a_ps.append(ps)
-        w2_codes = deal("w2_codes", w2_raw)
-        x_two = sb("x_two", [P, V], U32)
-        nc.vector.tensor_copy(x_two[:], xw_win[:].indirect(two_l[:]))
-        b_ps = []
-        for t in range(PLANES):
+            return ps
+
+        def project_b(t):
             ps = psum.tile([P, V], F32, name=f"b_ps{t}", tag=f"b{t}")
             nc.tensor.matmul_mx(
                 out=ps[:], lhsT=w2_codes[:, t * P : (t + 1) * P].bitcast(FP8X4), lhsT_scale=w_plane[:, t * P : (t + 1) * P],
                 rhs=x_two[:].bitcast(FP8X4), rhs_scale=x_plane[:, :V], start=True, stop=True,
             )
-            b_ps.append(ps)
+            return ps
+
+        b_ps = [project_b(t) for t in (0, 1)]
+        a_ps = [project_a(t) for t in range(PLANES)]
+        b_ps.extend(project_b(t) for t in (2, 3))
 
         z2_f = sb("z2_f", [P, PLANES, V], F32)
         z_pl = sb("z_pl", [P, PLANES, S], BF16)
@@ -152,7 +158,7 @@ def tile_picked_hkqhopmncubelse_none_po_kernel(
 
         def a_fetch(t):
             a_win = sb(f"a_win{t}", [P, 2 * S], F32)
-            if t < 2:
+            if t == PLANES - 1:
                 nc.scalar.activation(a_win[:, :S], a_ps[t][:], ACT.Copy, scale=ga_abs[:, t : t + 1])
             else:
                 nc.vector.tensor_scalar(a_win[:, :S], a_ps[t][:], ga_abs[:, t : t + 1], None, ALU.mult)
@@ -167,8 +173,11 @@ def tile_picked_hkqhopmncubelse_none_po_kernel(
 
         def st_fetch(t, st_win):
             st2 = sb(f"st2_{t}", [P, S], F32)
-            if t < 2:
+            if t == 0:
                 nc.vector.tensor_copy(st2[:], st_win[:].indirect(n2_l[:]))
+            elif t == 1:
+                nc.scalar.activation(st2[:, : S // 2], st_win[:].indirect(n2_l[:, : S // 32]), ACT.Copy)
+                nc.vector.tensor_copy(st2[:, S // 2 :], st_win[:].indirect(n2_l[:, S // 32 :]))
             else:
                 nc.scalar.activation(st2[:], st_win[:].indirect(n2_l[:]), ACT.Copy)
             return st2
@@ -181,38 +190,26 @@ def tile_picked_hkqhopmncubelse_none_po_kernel(
                 ALU.min,
             )
 
-        a_got, b_got, st, st2 = {}, {}, {}, {}
-        a_got[0] = a_fetch(0)
-        b_got[0] = b_fetch(0)
-        for t in (1, 2):
-            a_got[t] = a_fetch(t)
-            b_product(t - 1, *b_got[t - 1])
-            st[t - 1] = a_max(t - 1, *a_got[t - 1])
-            if t == 1:
-                b_got[1] = b_fetch(1)
-        a_got[3] = a_fetch(3)
-        b_got[2] = b_fetch(2)
-        st[2] = a_max(2, *a_got[2])
-        b_product(2, *b_got[2])
-        st[3] = a_max(3, *a_got[3])
-        b_got[3] = b_fetch(3)
-        st2[0] = st_fetch(0, st[0])
-        b_product(3, *b_got[3])
-        st2[1] = st_fetch(1, st[1])
-        st_min(0, st[0], st2[0])
-        st2[2] = st_fetch(2, st[2])
+        b_got = [b_fetch(t) for t in (0, 1)]
+        b_product(0, *b_got[0])
+        a_got = [a_fetch(t) for t in range(PLANES)]
+        b_product(1, *b_got[1])
+        st = [a_max(t, *a_got[t]) for t in range(PLANES)]
+        b_got.extend(b_fetch(t) for t in (2, 3))
+        st2 = [st_fetch(t, st[t]) for t in range(PLANES)]
+        for t in (2, 3):
+            b_product(t, *b_got[t])
         z2_bf = sb("z2_bf", [P, V * PLANES], BF16)
         nc.scalar.copy(
             z2_bf[:].rearrange("p (c i t) -> p c t i", i=4, t=PLANES),
             z2_f[:].rearrange("p t (c i) -> p c t i", i=4),
         )
-        st_min(1, st[1], st2[1])
-        st2[3] = st_fetch(3, st[3])
+        st_min(0, st[0], st2[0])
         z2_codes = sb("z2_codes", [P, V], U32)
         z2_plane = sb("z2_plane", [P, V], U8)
         nc.vector.quantize_mx(out=z2_codes[:].bitcast(FP8X4), scales=z2_plane[:], in_=z2_bf[:])
-        st_min(2, st[2], st2[2])
-        st_min(3, st[3], st2[3])
+        for t in range(1, PLANES):
+            st_min(t, st[t], st2[t])
 
         total = sb("total", [P, PLANES, V], F32)
         s_wins = []

from contextlib import ExitStack

import concourse.mybir as mybir
from concourse.masks import make_identity

F32 = mybir.dt.float32
BF16 = mybir.dt.bfloat16
I32 = mybir.dt.int32
U32 = mybir.dt.uint32
U16 = mybir.dt.uint16
U8 = mybir.dt.uint8
FP8X4 = mybir.dt.float8_e4m3fn_x4
ALU = mybir.AluOpType
ACT = mybir.ActivationFunctionType

P = 128
T = 2048
S = 512
V = 256
H = 512
PLANES = 4
V_WINDOW = V + 16
FLOPS = 2 * 512 * H * S + 2 * 512 * H * V + 2 * H * S * V


def tile_picked_hkqhopmncubelse_none_po_kernel(
    tc, x_words, x_scales, w1_words, w1_scales, w2_words, w2_scales, ga, gb,
    offs, two, n1, n2, n3, n4, n5, n6, out_0, out_1, out_2,
):
    nc = tc.nc
    with ExitStack() as ctx:
        pool = ctx.enter_context(tc.tile_pool(name="pool", bufs=1))
        psum = ctx.enter_context(tc.psum_pool(name="psum", bufs=1))

        def sb(name, shape, dtype):
            return pool.tile(shape, dtype, name=name, align_bytes=64)

        def load_list(name, src):
            t = sb(name, list(src.shape), U16)
            nc.sync.dma_start(t[:], src)
            return t

        def words_of(src):
            return src[0].rearrange("p n t -> p (n t)").bitcast(I32)

        xs_win = sb("xs_win", [P, T], U8)
        nc.gpsimd.memset(xs_win[:, : T // 2].bitcast(I32), 0)
        nc.vector.memset(xs_win[:, T // 2 :].bitcast(I32), 0)
        ws_raw = sb("ws_raw", [P, 2, H // 4], I32)
        nc.vector.memset(ws_raw[:], 0)
        g_raw = sb("g_raw", [2, H], F32)
        for i, g in enumerate((ga, gb)):
            nc.scalar.dma_start(g_raw[i : i + 1, :], g.rearrange("h o -> o h"))
        nc.scalar.dma_start(xs_win[0:P:8, :].bitcast(I32), x_scales[0].bitcast(I32))
        two_l = load_list("two_l", two)
        offs_l = load_list("offs_l", offs)
        nc.sync.dma_start(ws_raw[0:P:8, 1, :], w1_scales[0].bitcast(I32))
        nc.sync.dma_start(ws_raw[0:P:8, 0, :], w2_scales[0].bitcast(I32))
        xw_win = sb("xw_win", [P, T], U32)
        nc.sync.dma_start(xw_win[:].bitcast(I32), words_of(x_words))
        n1_l = load_list("n1_l", n1)
        n3_l = load_list("n3_l", n3)
        n4_l = load_list("n4_l", n4)
        w2_raw = sb("w2_raw", [P, H], I32)
        nc.sync.dma_start(w2_raw[:], words_of(w2_words))
        w1_raw = sb("w1_raw", [P, H], I32)
        nc.sync.dma_start(w1_raw[:], words_of(w1_words))
        n2_l = load_list("n2_l", n2)
        n5_l = load_list("n5_l", n5)
        n6_l = load_list("n6_l", n6)

        g_rows = sb("g_rows", [P, H], F32)
        nc.vector.memset(g_rows[:], 0.0)
        ident = sb("ident", [P, P], F32)
        make_identity(nc, ident[:])
        nc.scalar.copy(
            g_rows[0:2, :].rearrange("p (t a b) -> p a t b", t=PLANES, b=8),
            g_raw[:].rearrange("p (a t b) -> p a t b", t=PLANES, b=8),
        )

        xs_got = sb("xs_got", [P, V + S], U8)
        nc.vector.tensor_copy(xs_got[:, :V], xs_win[:].indirect(two_l[:]))
        nc.vector.tensor_copy(xs_got[:, V:], xs_win[:].indirect(offs_l[:]))
        planes = sb("planes", [P, V + S + 2 * H], U8)
        x_plane = planes[:, : V + S]
        w_plane = planes[:, V + S :]
        nc.gpsimd.tensor_copy(
            w_plane.bitcast(I32).rearrange("p (w t a b) -> p w a t b", w=2, t=PLANES, b=2),
            ws_raw[:].rearrange("p w (a t b) -> p w a t b", t=PLANES, b=2),
        )
        nc.vector.tensor_copy(x_plane.bitcast(I32), xs_got[:].bitcast(I32))
        for i in range(1, 4):
            nc.scalar.dma_start(planes[i:P:32, :].bitcast(I32), planes[8 * i : P : 32, :].bitcast(I32))

        g_ps = psum.tile([P, PLANES, P], F32, name="g_ps", tag="b0")
        for t in range(PLANES):
            nc.tensor.transpose(g_ps[:, t, :], g_rows[:, t * P : (t + 1) * P], ident[:])
        ga_abs = sb("ga_abs", [P, PLANES], F32)
        ga_sign = sb("ga_sign", [P, PLANES], F32)
        gb_signed = sb("gb_signed", [P, PLANES], F32)
        nc.scalar.activation(ga_abs[:], g_ps[:, :, 0], ACT.Abs)
        nc.scalar.activation(ga_sign[:], g_ps[:, :, 0], ACT.Sign)
        gb_dealt = sb("gb_dealt", [P, PLANES], F32)
        nc.scalar.copy(gb_dealt[:], g_ps[:, :, 1])
        nc.gpsimd.tensor_tensor(gb_signed[:], gb_dealt[:], ga_sign[:], ALU.mult)

        def deal(name, raw):
            dealt = sb(name, [P, H], U32)
            nc.vector.tensor_copy(
                dealt[:].bitcast(I32).rearrange("p (t a b) -> p a t b", t=PLANES, b=8),
                raw[:].rearrange("p (a t b) -> p a t b", t=PLANES, b=8),
            )
            return dealt

        x_two = sb("x_two", [P, V], U32)
        nc.vector.tensor_copy(x_two[:], xw_win[:].indirect(two_l[:]))
        w2_codes = deal("w2_codes", w2_raw)
        x_offs = sb("x_offs", [P, S], U32)
        nc.vector.tensor_copy(x_offs[:], xw_win[:].indirect(offs_l[:]))
        w1_codes = deal("w1_codes", w1_raw)

        def project_a(t):
            ps = psum.tile([P, S], F32, name=f"a_ps{t}", tag=f"a{t}")
            nc.tensor.matmul_mx(
                out=ps[:], lhsT=w1_codes[:, t * P : (t + 1) * P].bitcast(FP8X4), lhsT_scale=w_plane[:, H + t * P : H + (t + 1) * P],
                rhs=x_offs[:].bitcast(FP8X4), rhs_scale=x_plane[:, V:], start=True, stop=True,
            )
            return ps

        def project_b(t):
            ps = psum.tile([P, V], F32, name=f"b_ps{t}", tag=f"b{t}")
            nc.tensor.matmul_mx(
                out=ps[:], lhsT=w2_codes[:, t * P : (t + 1) * P].bitcast(FP8X4), lhsT_scale=w_plane[:, t * P : (t + 1) * P],
                rhs=x_two[:].bitcast(FP8X4), rhs_scale=x_plane[:, :V], start=True, stop=True,
            )
            return ps

        b_ps = [project_b(t) for t in (0, 1)]
        a_ps = [project_a(t) for t in range(PLANES)]
        b_ps.extend(project_b(t) for t in (2, 3))

        z2_f = sb("z2_f", [P, PLANES, V], F32)
        z_pl = sb("z_pl", [P, PLANES, S], BF16)

        def b_fetch(t):
            b_win = sb(f"b_win{t}", [P, V_WINDOW], F32)
            nc.scalar.activation(b_win[:, :V], b_ps[t][:], ACT.Copy, scale=gb_signed[:, t : t + 1])
            tanh_win = sb(f"tanh_win{t}", [P, V_WINDOW], F32)
            nc.scalar.activation(tanh_win[:, :V], b_ps[t][:], ACT.Tanh)
            b3 = sb(f"b3_{t}", [P, V], F32)
            nc.scalar.activation(b3[:], b_win[:].indirect(n3_l[:]), ACT.Copy)
            return tanh_win, b3

        def b_product(t, tanh_win, b3):
            bb = sb(f"bb{t}", [P, V], F32)
            nc.vector.tensor_tensor(bb[:], b_ps[t][:], b3[:], ALU.mult)
            nc.vector.tensor_tensor(z2_f[:, t, :], tanh_win[:].indirect(n4_l[:]), bb[:], ALU.mult)

        def a_fetch(t):
            a_win = sb(f"a_win{t}", [P, 2 * S], F32)
            if t == PLANES - 1:
                nc.scalar.activation(a_win[:, :S], a_ps[t][:], ACT.Copy, scale=ga_abs[:, t : t + 1])
            else:
                nc.vector.tensor_scalar(a_win[:, :S], a_ps[t][:], ga_abs[:, t : t + 1], None, ALU.mult)
            a1 = sb(f"a1_{t}", [P, S], F32)
            nc.scalar.activation(a1[:], a_win[:].indirect(n1_l[:]), ACT.Copy)
            return a_win, a1

        def a_max(t, a_win, a1):
            st_win = sb(f"st_win{t}", [P, 2 * S], F32)
            nc.vector.tensor_tensor(st_win[:, :S], a_win[:, :S], a1[:], ALU.max)
            return st_win

        def st_fetch(t, st_win):
            st2 = sb(f"st2_{t}", [P, S], F32)
            if t == 0:
                nc.vector.tensor_copy(st2[:], st_win[:].indirect(n2_l[:]))
            elif t == 1:
                nc.scalar.activation(st2[:, : S // 2], st_win[:].indirect(n2_l[:, : S // 32]), ACT.Copy)
                nc.vector.tensor_copy(st2[:, S // 2 :], st_win[:].indirect(n2_l[:, S // 32 :]))
            else:
                nc.scalar.activation(st2[:], st_win[:].indirect(n2_l[:]), ACT.Copy)
            return st2

        def st_min(t, st_win, st2):
            nc.vector.tensor_tensor(
                z_pl[:, t, :].rearrange("p (u m) -> p m u", u=PLANES),
                st_win[:, :S].rearrange("p (m u) -> p m u", u=PLANES),
                st2[:].rearrange("p (m u) -> p m u", u=PLANES),
                ALU.min,
            )

        b_got = [b_fetch(t) for t in (0, 1)]
        b_product(0, *b_got[0])
        a_got = [a_fetch(t) for t in range(PLANES)]
        b_product(1, *b_got[1])
        st = [a_max(t, *a_got[t]) for t in range(PLANES)]
        b_got.extend(b_fetch(t) for t in (2, 3))
        st2 = [st_fetch(t, st[t]) for t in range(PLANES)]
        for t in (2, 3):
            b_product(t, *b_got[t])
        z2_bf = sb("z2_bf", [P, V * PLANES], BF16)
        nc.scalar.copy(
            z2_bf[:].rearrange("p (c i t) -> p c t i", i=4, t=PLANES),
            z2_f[:].rearrange("p t (c i) -> p c t i", i=4),
        )
        st_min(0, st[0], st2[0])
        z2_codes = sb("z2_codes", [P, V], U32)
        z2_plane = sb("z2_plane", [P, V], U8)
        nc.vector.quantize_mx(out=z2_codes[:].bitcast(FP8X4), scales=z2_plane[:], in_=z2_bf[:])
        for t in range(1, PLANES):
            st_min(t, st[t], st2[t])

        total = sb("total", [P, PLANES, V], F32)
        s_wins = []
        z_bfs = []
        for u in range(PLANES):
            z_bf = sb(f"z_bf{u}", [P, P * PLANES], BF16)
            z_bfs.append(z_bf)

        def weave(u):
            copy = nc.scalar.copy if u == 1 else nc.vector.tensor_copy
            copy(
                z_bfs[u][:].rearrange("p (c i t) -> p c t i", i=4, t=PLANES),
                z_pl[:, :, u * P : (u + 1) * P].rearrange("p t (c i) -> p c t i", i=4),
            )

        def scores(u):
            z_codes = sb(f"z_codes{u}", [P, P], U32)
            z_plane = sb(f"z_plane{u}", [P, P], U8)
            nc.vector.quantize_mx(out=z_codes[:].bitcast(FP8X4), scales=z_plane[:], in_=z_bfs[u][:])
            ps = psum.tile([P, V], F32, name=f"s_ps{u}", tag=f"b{u}")
            nc.tensor.matmul_mx(
                out=ps[:], lhsT=z_codes[:].bitcast(FP8X4), lhsT_scale=z_plane[:],
                rhs=z2_codes[:].bitcast(FP8X4), rhs_scale=z2_plane[:], start=True, stop=True,
            )
            ex_win = sb(f"ex_win{u}", [P, 2 * V], F32)
            nc.scalar.activation(ex_win[:, :V], ps[:], ACT.Exp, scale=0.0625)
            ex5 = sb(f"ex5_{u}", [P, V], F32)
            nc.scalar.activation(ex5[:], ex_win[:].indirect(n5_l[:]), ACT.Copy)
            return ps, ex_win, ex5

        sc = []
        for pair in (0, 2):
            weave(pair)
            weave(pair + 1)
            sc.append(scores(pair))
            sc.append(scores(pair + 1))
        for u in range(PLANES):
            s_win = sb(f"s_win{u}", [P, 2 * V], F32)
            nc.vector.tensor_scalar(s_win[:, :V], sc[u][0][:], 0.0625, None, ALU.mult)
            s_wins.append(s_win)
        for u in range(PLANES):
            nc.vector.tensor_tensor(total[:, u, :], sc[u][1][:, :V], sc[u][2][:], ALU.add)
        log_total = sb("log_total", [P, PLANES, V], F32)
        nc.scalar.activation(log_total[:], total[:], ACT.Ln)
        out_rows = out_0.rearrange("(p u) v -> p u v", u=PLANES)
        result = sb("result", [P, PLANES, V], F32)
        out_bf = sb("out_bf", [P, V, PLANES], BF16)
        out_codes = sb("out_codes", [P, V], U32)
        out_plane = sb("out_plane", [P, V], U8)

        def finish(u, cols):
            s6 = sc[PLANES - 1][2][:, cols] if u == 0 else total[:, u, cols]
            nc.scalar.activation(s6, s_wins[u][:].indirect(n6_l[:, cols.start // 16 : cols.stop // 16]), ACT.Copy)
            nc.vector.tensor_tensor(result[:, u, cols], log_total[:, u, cols], s6, ALU.subtract)

        def round_pair(u, cols):
            nc.vector.tensor_copy(out_bf[:, cols, u : u + 2], result[:, u : u + 2, cols].rearrange("p u v -> p v u"))

        for u in range(PLANES - 1):
            finish(u, slice(0, V))
            nc.sync.dma_start(out_rows[:, u, :], result[:, u, :])
            if u == 1:
                round_pair(0, slice(0, V))
        for cols in (slice(0, V // 2), slice(V // 2, V)):
            finish(PLANES - 1, cols)
            round_pair(2, cols)
            nc.vector.quantize_mx(
                out=out_codes[:, cols].bitcast(FP8X4), scales=out_plane[:, cols],
                in_=out_bf[:, cols, :].rearrange("p v u -> p (v u)"),
            )
        nc.sync.dma_start(out_rows[:, PLANES - 1, :], result[:, PLANES - 1, :])
        nc.sync.dma_start(words_of(out_1), out_codes[:].bitcast(I32))
        for q in range(4):
            queue = nc.sync if q % 2 == 0 else nc.scalar
            queue.dma_start(out_2[0, 4 * q : 4 * q + 4, :].bitcast(I32), out_plane[32 * q : 32 * q + 4, :].bitcast(I32))
